import numpy as np
import ml_dtypes


def mxq(x, axis, fmt="e4m3"):
    dtype, down = {"e4m3": (ml_dtypes.float8_e4m3fn, 7), "e5m2": (ml_dtypes.float8_e5m2, 14)}[fmt]
    v = np.moveaxis(np.asarray(x, np.float32).astype(ml_dtypes.bfloat16).astype(np.float64), axis, -1)
    blocks = v.reshape(v.shape[:-1] + (-1, 32))
    amax = np.abs(blocks).max(-1, keepdims=True)
    byte = np.maximum(np.where(amax > 0, np.frexp(amax)[1] - 1 + 127, 0) - down, 1)
    scale = np.exp2(byte - 127.0)
    codes = (blocks / scale).astype(np.float32).astype(dtype).astype(np.float64)
    return np.moveaxis((codes * scale).reshape(v.shape), -1, axis)


WIDE = False


def mx_kscale(k):
    if not WIDE:
        return np.ones(k)
    levels = np.array([10, -10, 5, -5, 0])
    if k % 512:
        return np.exp2(np.random.permutation(np.resize(levels, k // 32))).repeat(32)
    a = np.empty((k // 512, 16))
    for p in range(k // 512):
        a[p, :8] = np.random.permutation(np.resize(levels, 8))
        for g in range(8):
            far = levels[np.abs(levels - a[p, g]) >= 10]
            a[p, g + 8] = far[np.random.randint(len(far))]
    return np.exp2(a.ravel()).repeat(32)


BF16 = ml_dtypes.bfloat16


def bf(x):
    return np.asarray(x, np.float32).astype(BF16)


def f64(x):
    return np.asarray(x).astype(np.float64)


T, D, H, NA, NB, V = 8192, 512, 4, 32, 32, 128
NSLOT = NA * NB


def draw0():
    s = mx_kscale(D)
    t = mx_kscale(NSLOT).reshape(NA, NB)
    root_d = np.sqrt(D)
    return {
        "x": bf(np.random.standard_normal((T, D)) * s),
        "ka": bf(1.5 * np.random.standard_normal((D, H, NA)) / root_d / s[:, None, None]),
        "kb": bf(1.5 * np.random.standard_normal((D, H, NB)) / root_d / s[:, None, None]),
        "gs": bf(16.0 * np.random.standard_normal((NA, NB)) * t),
        "vals": bf(0.25 * np.random.standard_normal((NA, NB, V)) / t[:, :, None]),
        "wg": bf(np.random.standard_normal((D, V)) / root_d / s[:, None]),
    }


def softmax(v):
    e = np.exp(v - v.max(axis=-1, keepdims=True))
    return e / e.sum(axis=-1, keepdims=True)


def head_logits(xq, keys):
    d, h, n = keys.shape
    flat = xq @ mxq(keys.reshape(d, h * n), 0, "e4m3")
    return flat.reshape(xq.shape[0], h, n)


def outer_over_heads(a, b):
    w = a[:, 0, :, None] * b[:, 0, None, :]
    for h in range(1, a.shape[1]):
        w = w + a[:, h, :, None] * b[:, h, None, :]
    return w


def core(x, ka, kb, gs, vals, wg):
    x, ka, kb, gs, vals, wg = f64(x), f64(ka), f64(kb), f64(gs), f64(vals), f64(wg)
    t = x.shape[0]
    na, nb, v = vals.shape
    xq = mxq(x, 1, "e4m3")

    la = head_logits(xq, ka)
    lb = head_logits(xq, kb)

    a = softmax(la)
    b = softmax(lb)

    w = outer_over_heads(a, b)

    u = w * gs[None, :, :]

    r = mxq(u.reshape(t, na * nb), 1, "e4m3") @ mxq(vals.reshape(na * nb, v), 0, "e4m3")

    z = xq @ mxq(wg, 0, "e4m3")

    return r * z * (1.0 / (1.0 + np.exp(-z)))


def e4m3fn_bytes(y):
    return np.clip(np.asarray(y, np.float64), -448.0, 448.0).astype(np.float32).astype(ml_dtypes.float8_e4m3fn).view(np.uint8)


def e4m3fn_values(b):
    return np.asarray(b, np.uint8).view(ml_dtypes.float8_e4m3fn).astype(np.float64)


def setup_inputs():
    d = draw0()
    x0 = np.asarray(d['x']).astype(np.float64)
    s = (np.max(np.abs(x0), axis=(0,), keepdims=True) / 448.0).astype(np.float32)
    out = {}
    for k, v in d.items():
        if k == 'x':
            out['x_bytes'] = e4m3fn_bytes(x0 / s.astype(np.float64))
            out['x_scale'] = s
        else:
            out[k] = v
    return out


def reference(x_bytes, x_scale, ka, kb, gs, vals, wg):
    return core(e4m3fn_values(x_bytes) * x_scale.astype(np.float64), ka, kb, gs, vals, wg)

@@ -1,0 +1,254 @@
+from contextlib import ExitStack
+
+import concourse.mybir as mybir
+from concourse.masks import make_identity
+
+T, D, H, NA, NB, V = 8192, 512, 4, 32, 32, 128
+FLOPS = 2 * T * D * (H * NA + H * NB + V) + 2 * T * NA * NB * V
+
+F32 = mybir.dt.float32
+BF16 = mybir.dt.bfloat16
+U32 = mybir.dt.uint32
+U8 = mybir.dt.uint8
+FP8 = mybir.dt.float8_e4m3fn
+FP8X4 = mybir.dt.float8_e4m3fn_x4
+ALU = mybir.AluOpType
+ACT = mybir.ActivationFunctionType
+AX = mybir.AxisListType
+
+P = 128
+PACK = 4
+R = NB // PACK
+G = 2
+IG = NA // G
+NT = T // P
+CH = 4
+KEYS = H * NA + H * NB
+
+
+def tile_denseproductkeymemorygated_t_kernel(tc, x_bytes, x_scale, ka, kb, gs, vals, wg, out):
+    nc = tc.nc
+    with ExitStack() as ctx:
+        keep = ctx.enter_context(tc.tile_pool(name="keep", bufs=1))
+        xin = ctx.enter_context(tc.tile_pool(name="xin", bufs=NT // CH))
+        work = ctx.enter_context(tc.tile_pool(name="work", bufs=3))
+        gate_pool = ctx.enter_context(tc.tile_pool(name="gate", bufs=6))
+        ps1 = ctx.enter_context(tc.psum_pool(name="ps1", bufs=1))
+        ps2 = ctx.enter_context(tc.psum_pool(name="ps2", bufs=2))
+        ps3 = ctx.enter_context(tc.psum_pool(name="ps3", bufs=3))
+        ctx.enter_context(tc.manual_schedule())
+
+        xraw = {}
+
+        def load_x(c):
+            xraw[c] = xin.tile([P, CH, D], U8, name="xraw")
+            nc.sync.dma_start(out=xraw[c][:], in_=x_bytes[c * CH * P:(c + 1) * CH * P, :].rearrange("(p q) k -> p q k", q=CH))
+
+        load_x(0)
+        xs = keep.tile([P, PACK], F32, name="xs")
+        nc.sync.dma_start(out=xs[:], in_=x_scale.rearrange("o (p t) -> p (o t)", t=PACK))
+        ka_raw = keep.tile([P, PACK, H * NA], BF16, name="ka_raw")
+        nc.sync.dma_start(out=ka_raw[:], in_=ka.rearrange("(p t) h i -> p t (h i)", t=PACK))
+        kb_raw = keep.tile([P, PACK, H * NB], BF16, name="kb_raw")
+        nc.sync.dma_start(out=kb_raw[:], in_=kb.rearrange("(p t) h j -> p t (h j)", t=PACK))
+        wg_raw = keep.tile([P, PACK, V], BF16, name="wg_raw")
+        nc.sync.dma_start(out=wg_raw[:], in_=wg.rearrange("(p t) v -> p t v", t=PACK))
+        vals_raw = keep.tile([P, G, PACK * V], BF16, name="vals_raw")
+        nc.sync.dma_start(out=vals_raw[:], in_=vals.rearrange("i j v -> (i j) v").rearrange("(g p t) v -> p g (t v)", g=G, t=PACK))
+        gain = keep.tile([P, G, PACK], BF16, name="gain")
+        nc.sync.dma_start(out=gain[:], in_=gs.rearrange("i j -> (i j)").rearrange("(g p t) -> p g t", g=G, t=PACK))
+        for c in range(1, NT // CH):
+            load_x(c)
+
+        ident = keep.tile([P, P], F32, name="ident")
+        make_identity(nc, ident[:])
+
+        w_grp = keep.tile([P, KEYS + V, PACK], BF16, name="w_grp", align_bytes=64)
+        nc.vector.tensor_copy(out=w_grp[:, 0:H * NA, :], in_=ka_raw[:].rearrange("p t c -> p c t"))
+        nc.vector.tensor_copy(
+            out=w_grp[:, H * NA:KEYS, :].rearrange("p (h s r) t -> p h s r t", h=H, s=PACK),
+            in_=kb_raw[:].rearrange("p t (h r s) -> p h s r t", h=H, s=PACK),
+        )
+        nc.vector.tensor_copy(out=w_grp[:, KEYS:KEYS + V, :], in_=wg_raw[:].rearrange("p t c -> p c t"))
+        w_codes = keep.tile([P, KEYS + V], U32, name="w_codes", align_bytes=64)
+        w_scales = keep.tile([P, KEYS + V], U8, name="w_scales", align_bytes=64)
+        for lo, hi in ((0, KEYS), (KEYS, KEYS + V)):
+            nc.vector.quantize_mx(out=w_codes[:, lo:hi].bitcast(FP8X4), scales=w_scales[:, lo:hi],
+                                  in_=w_grp[:, lo:hi, :].rearrange("p c t -> p (c t)"))
+        v_grp = keep.tile([P, G, V, PACK], BF16, name="v_grp", align_bytes=64)
+        v_codes = keep.tile([P, G * V], U32, name="v_codes", align_bytes=64)
+        v_scales = keep.tile([P, G * V], U8, name="v_scales", align_bytes=64)
+
+        def quantise_vals():
+            nc.vector.tensor_copy(out=v_grp[:], in_=vals_raw[:].rearrange("p g (t v) -> p g v t", t=PACK))
+            nc.vector.quantize_mx(out=v_codes[:].bitcast(FP8X4), scales=v_scales[:],
+                                  in_=v_grp[:].rearrange("p g v t -> p (g v t)"))
+
+        xw, xt, xb, xq, xqs, lg, nm, e, sm, th, gt, cc, rc, an, bps = ({} for unused in range(15))
+        prod, wt, ub, uq, uqs, rr, ot = ({} for unused in range(7))
+
+        def widen(n):
+            xw[n] = work.tile([P, D], BF16, name="xw")
+            nc.scalar.copy(out=xw[n][:], in_=xraw[n // CH][:, n % CH, :].bitcast(FP8))
+
+        def turn_x(n):
+            xt[n] = ps1.tile([P, 2, P], F32, name="xt")
+            words = xw[n][:].bitcast(F32)
+            for u in range(2):
+                nc.tensor.transpose(xt[n][:, u, :], words[:, u:D // 2:2], ident[:])
+
+        def scale_x(n):
+            xb[n] = work.tile([P, P, 2, 2], BF16, name="xb", align_bytes=64)
+            nc.vector.tensor_tensor(
+                out=xb[n][:],
+                in0=xt[n][:].rearrange("p u k -> p (u k)").bitcast(BF16).rearrange("p (u k e) -> p k u e", u=2, e=2),
+                in1=xs[:].rearrange("p (u e) -> p u e", u=2).unsqueeze(1).to_broadcast([P, P, 2, 2]),
+                op=ALU.mult)
+
+        def quantise_x(n):
+            xq[n] = work.tile([P, P], U32, name="xq", align_bytes=64)
+            xqs[n] = work.tile([P, P], U8, name="xqs", align_bytes=64)
+            nc.vector.quantize_mx(out=xq[n][:].bitcast(FP8X4), scales=xqs[n][:],
+                                  in_=xb[n][:].rearrange("p k u e -> p (k u e)"))
+
+        def logits(n):
+            lg[n] = ps2.tile([P, KEYS + V], F32, name="lg")
+            for lo, hi in ((0, KEYS), (KEYS, KEYS + V)):
+                nc.tensor.matmul_mx(out=lg[n][:, lo:hi], lhsT=xq[n][:].bitcast(FP8X4), lhsT_scale=xqs[n][:],
+                                    rhs=w_codes[:, lo:hi].bitcast(FP8X4), rhs_scale=w_scales[:, lo:hi],
+                                    start=True, stop=True)
+
+        def row_max(n):
+            nm[n] = work.tile([P, 2 * H], F32, name="nm")
+            nc.vector.tensor_reduce(out=nm[n][:], in_=lg[n][:, 0:KEYS].rearrange("p (h i) -> p h i", i=NA),
+                                    axis=AX.X, op=ALU.max, negate=True)
+
+        def exps(n):
+            e[n] = work.tile([P, KEYS], F32, name="e")
+            sm[n] = work.tile([P, 2 * H], F32, name="sm")
+            for h in range(2 * H):
+                cols = slice(h * NA, (h + 1) * NA)
+                nc.scalar.activation(out=e[n][:, cols], in_=lg[n][:, cols], func=ACT.Exp, bias=nm[n][:, h:h + 1],
+                                     accum_out=sm[n][:, h:h + 1])
+            th[n] = work.tile([P, V], F32, name="th")
+            nc.scalar.activation(out=th[n][:], in_=lg[n][:, KEYS:KEYS + V], func=ACT.Tanh, scale=0.5)
+
+        def gate(n):
+            gt[n] = gate_pool.tile([P, V], F32, name="gt")
+            nc.vector.scalar_tensor_tensor(out=gt[n][:], in0=th[n][:], scalar=1.0, in1=lg[n][:, KEYS:KEYS + V],
+                                           op0=ALU.add, op1=ALU.mult)
+
+        def sum_product(n):
+            cc[n] = work.tile([P, H], F32, name="cc")
+            nc.vector.tensor_tensor(out=cc[n][:], in0=sm[n][:, 0:H], in1=sm[n][:, H:2 * H], op=ALU.mult)
+
+        def invert(n):
+            rc[n] = work.tile([P, H], F32, name="rc")
+            nc.vector.reciprocal(out=rc[n][:], in_=cc[n][:])
+
+        def normalise(n):
+            an[n] = work.tile([P, H, NA], F32, name="an")
+            nc.vector.tensor_tensor(out=an[n][:], in0=e[n][:, 0:H * NA].rearrange("p (h i) -> p h i", h=H),
+                                    in1=rc[n][:].unsqueeze(2).to_broadcast([P, H, NA]), op=ALU.mult)
+
+        def b_to_psum(n):
+            bps[n] = ps1.tile([P, 2 * NB], F32, name="bps")
+            nc.tensor.matmul(out=bps[n][:], lhsT=ident[:], rhs=e[n][:, H * NA:H * NA + 2 * NB], start=True, stop=True)
+
+        def outer(engine, n, name, b_cols, h, i0, i1, t0, t1):
+            shape = [P, t1 - t0, i1 - i0, R]
+            tl = work.tile(shape, F32, name=name)
+            engine.tensor_tensor(
+                out=tl[:],
+                in0=b_cols[:, t0 * R:t1 * R].rearrange("p (t r) -> p t r", r=R).unsqueeze(2).to_broadcast(shape),
+                in1=an[n][:, h, i0:i1].unsqueeze(1).unsqueeze(3).to_broadcast(shape),
+                op=ALU.mult)
+            for g in range(i0 // IG, i1 // IG):
+                for t in range(t0, t1):
+                    prod[n, h, g, t] = tl[:, t - t0, g * IG - i0:(g + 1) * IG - i0, :].rearrange("p i r -> p (i r)")
+
+        def b_of(n, h):
+            return e[n][:, H * NA + h * NB:H * NA + (h + 1) * NB]
+
+        def outer_gpsimd(n):
+            outer(nc.gpsimd, n, "p3", b_of(n, 3), 3, 0, NA, 0, PACK)
+            outer(nc.gpsimd, n, "p1g", b_of(n, 1), 1, IG, NA, 0, 2)
+
+        def outer_vector(n):
+            outer(nc.vector, n, "p0", bps[n][:, 0:NB], 0, 0, NA, 0, PACK)
+            outer(nc.vector, n, "p1v", bps[n][:, NB:2 * NB], 1, IG, NA, 2, PACK)
+
+        def outer_scalar(n):
+            for name, h, g in (("p1s", 1, 0), ("p2a", 2, 0), ("p2b", 2, 1)):
+                tl = work.tile([P, PACK, IG, R], F32, name=name)
+                for i in range(IG):
+                    nc.scalar.activation(out=tl[:, :, i, :], in_=b_of(n, h).rearrange("p (t r) -> p t r", r=R),
+                                         func=ACT.Copy, scale=an[n][:, h, g * IG + i:g * IG + i + 1])
+                for t in range(PACK):
+                    prod[n, h, g, t] = tl[:, t, :, :].rearrange("p i r -> p (i r)")
+
+        def turn_w(n, g):
+            wt[n, g] = ps3.tile([P, PACK, P], F32, name="wt")
+            for t in range(PACK):
+                for h in range(H):
+                    nc.tensor.matmul(out=wt[n, g][:, t, :], lhsT=prod[n, h, g, t], rhs=ident[:],
+                                     is_transpose=True, start=(h == 0), stop=(h == H - 1))
+
+        def apply_gain(n, g):
+            if g == 0:
+                ub[n] = work.tile([P, G, P, PACK], BF16, name="ub", align_bytes=64)
+            nc.vector.tensor_tensor(out=ub[n][:, g, :, :], in0=wt[n, g][:].rearrange("p t k -> p k t"),
+                                    in1=gain[:, g, :].unsqueeze(1).to_broadcast([P, P, PACK]), op=ALU.mult)
+
+        def quantise_u(n):
+            uq[n] = work.tile([P, G * P], U32, name="uq", align_bytes=64)
+            uqs[n] = work.tile([P, G * P], U8, name="uqs", align_bytes=64)
+            nc.vector.quantize_mx(out=uq[n][:].bitcast(FP8X4), scales=uqs[n][:],
+                                  in_=ub[n][:].rearrange("p g k t -> p (g k t)"))
+
+        def read_values(n):
+            rr[n] = ps1.tile([P, V], F32, name="rr")
+            for g in range(G):
+                nc.tensor.matmul_mx(out=rr[n][:], lhsT=uq[n][:, g * P:(g + 1) * P].bitcast(FP8X4),
+                                    lhsT_scale=uqs[n][:, g * P:(g + 1) * P],
+                                    rhs=v_codes[:, g * V:(g + 1) * V].bitcast(FP8X4), rhs_scale=v_scales[:, g * V:(g + 1) * V],
+                                    start=(g == 0), stop=(g == G - 1))
+
+        def finish(n):
+            c, q = divmod(n, CH)
+            if q == 0:
+                ot[c] = work.tile([P, CH, V], F32, name="ot")
+            nc.vector.scalar_tensor_tensor(out=ot[c][:, q, :], in0=rr[n][:], scalar=0.5, in1=gt[n][:],
+                                           op0=ALU.mult, op1=ALU.mult)
+            if q == CH - 1:
+                nc.sync.dma_start(out=out[c * CH * P:(c + 1) * CH * P, :].rearrange("(p q) v -> p q v", q=CH), in_=ot[c][:])
+
+        def on(stage, n, *more):
+            if 0 <= n < NT:
+                stage(n, *more)
+
+        for s in range(-4, NT + 3):
+            on(sum_product, s)
+            on(quantise_u, s - 3)
+            on(invert, s)
+            on(quantise_x, s + 2)
+            on(normalise, s)
+            if s == 0:
+                quantise_vals()
+            on(widen, s + 4)
+            on(outer_gpsimd, s)
+            on(logits, s + 1)
+            on(read_values, s - 3)
+            on(b_to_psum, s)
+            on(turn_x, s + 3)
+            on(row_max, s + 1)
+            on(exps, s + 1)
+            on(apply_gain, s - 2, 0)
+            on(turn_w, s - 1, 0)
+            on(apply_gain, s - 2, 1)
+            on(turn_w, s - 1, 1)
+            on(outer_vector, s)
+            on(outer_scalar, s)
+            on(scale_x, s + 3)
+            on(finish, s - 3)
+            on(gate, s + 1)

@@ -24,6 +24,7 @@ IG = NA // G
 NT = T // P
 CH = 4
 KEYS = H * NA + H * NB
+S_ROWS, V_ROWS = 12, 6
 
 
 def tile_denseproductkeymemorygated_t_kernel(tc, x_bytes, x_scale, ka, kb, gs, vals, wg, out):
@@ -140,7 +141,7 @@ def tile_denseproductkeymemorygated_t_kernel(tc, x_bytes, x_scale, ka, kb, gs, v
 
         def sum_product(n):
             cc[n] = work.tile([P, H], F32, name="cc")
-            nc.vector.tensor_tensor(out=cc[n][:], in0=sm[n][:, 0:H], in1=sm[n][:, H:2 * H], op=ALU.mult)
+            nc.vector.tensor_reduce(out=cc[n][:], in_=sm[n][:].rearrange("p (u h) -> p h u", u=2), axis=AX.X, op=ALU.mult)
 
         def invert(n):
             rc[n] = work.tile([P, H], F32, name="rc")
@@ -152,46 +153,43 @@ def tile_denseproductkeymemorygated_t_kernel(tc, x_bytes, x_scale, ka, kb, gs, v
                                     in1=rc[n][:].unsqueeze(2).to_broadcast([P, H, NA]), op=ALU.mult)
 
         def b_to_psum(n):
-            bps[n] = ps1.tile([P, 2 * NB], F32, name="bps")
-            nc.tensor.matmul(out=bps[n][:], lhsT=ident[:], rhs=e[n][:, H * NA:H * NA + 2 * NB], start=True, stop=True)
+            bps[n] = ps1.tile([P, H * NB], F32, name="bps")
+            nc.tensor.matmul(out=bps[n][:], lhsT=ident[:], rhs=e[n][:, H * NA:KEYS], start=True, stop=True)
 
-        def outer(engine, n, name, b_cols, h, i0, i1, t0, t1):
-            shape = [P, t1 - t0, i1 - i0, R]
-            tl = work.tile(shape, F32, name=name)
-            engine.tensor_tensor(
-                out=tl[:],
-                in0=b_cols[:, t0 * R:t1 * R].rearrange("p (t r) -> p t r", r=R).unsqueeze(2).to_broadcast(shape),
-                in1=an[n][:, h, i0:i1].unsqueeze(1).unsqueeze(3).to_broadcast(shape),
-                op=ALU.mult)
-            for g in range(i0 // IG, i1 // IG):
-                for t in range(t0, t1):
-                    prod[n, h, g, t] = tl[:, t - t0, g * IG - i0:(g + 1) * IG - i0, :].rearrange("p i r -> p (i r)")
+        def head_tile(n, h):
+            if (n, h) not in prod:
+                prod[n, h] = work.tile([P, PACK, NA, R], F32, name="prod%d" % h)
+            return prod[n, h]
 
         def b_of(n, h):
             return e[n][:, H * NA + h * NB:H * NA + (h + 1) * NB]
 
+        def outer(engine, n, h, b_cols, i0, i1):
+            shape = [P, PACK, i1 - i0, R]
+            engine.tensor_tensor(
+                out=head_tile(n, h)[:, :, i0:i1, :],
+                in0=b_cols.rearrange("p (t r) -> p t r", r=R).unsqueeze(2).to_broadcast(shape),
+                in1=an[n][:, h, i0:i1].unsqueeze(1).unsqueeze(3).to_broadcast(shape),
+                op=ALU.mult)
+
         def outer_gpsimd(n):
-            outer(nc.gpsimd, n, "p3", b_of(n, 3), 3, 0, NA, 0, PACK)
-            outer(nc.gpsimd, n, "p1g", b_of(n, 1), 1, IG, NA, 0, 2)
+            outer(nc.gpsimd, n, 3, b_of(n, 3), 0, NA)
+            outer(nc.gpsimd, n, 1, b_of(n, 1), S_ROWS + V_ROWS, NA)
 
         def outer_vector(n):
-            outer(nc.vector, n, "p0", bps[n][:, 0:NB], 0, 0, NA, 0, PACK)
-            outer(nc.vector, n, "p1v", bps[n][:, NB:2 * NB], 1, IG, NA, 2, PACK)
+            outer(nc.vector, n, 0, bps[n][:, 0:NB], 0, NA)
+            outer(nc.vector, n, 1, bps[n][:, NB:2 * NB], S_ROWS, S_ROWS + V_ROWS)
 
-        def outer_scalar(n):
-            for name, h, g in (("p1s", 1, 0), ("p2a", 2, 0), ("p2b", 2, 1)):
-                tl = work.tile([P, PACK, IG, R], F32, name=name)
-                for i in range(IG):
-                    nc.scalar.activation(out=tl[:, :, i, :], in_=b_of(n, h).rearrange("p (t r) -> p t r", r=R),
-                                         func=ACT.Copy, scale=an[n][:, h, g * IG + i:g * IG + i + 1])
-                for t in range(PACK):
-                    prod[n, h, g, t] = tl[:, t, :, :].rearrange("p i r -> p (i r)")
+        def outer_scalar(n, h, i0, i1):
+            for i in range(i0, i1):
+                nc.scalar.activation(out=head_tile(n, h)[:, :, i, :], in_=b_of(n, h).rearrange("p (t r) -> p t r", r=R),
+                                     func=ACT.Copy, scale=an[n][:, h, i:i + 1])
 
         def turn_w(n, g):
             wt[n, g] = ps3.tile([P, PACK, P], F32, name="wt")
             for t in range(PACK):
                 for h in range(H):
-                    nc.tensor.matmul(out=wt[n, g][:, t, :], lhsT=prod[n, h, g, t], rhs=ident[:],
+                    nc.tensor.matmul(out=wt[n, g][:, t, :], lhsT=prod[n, h][:, t, g * IG:(g + 1) * IG, :].rearrange("p i r -> p (i r)"), rhs=ident[:],
                                      is_transpose=True, start=(h == 0), stop=(h == H - 1))
 
         def apply_gain(n, g):
@@ -228,15 +226,14 @@ def tile_denseproductkeymemorygated_t_kernel(tc, x_bytes, x_scale, ka, kb, gs, v
                 stage(n, *more)
 
         for s in range(-4, NT + 3):
-            on(sum_product, s)
             on(quantise_u, s - 3)
-            on(invert, s)
             on(quantise_x, s + 2)
             on(normalise, s)
             if s == 0:
                 quantise_vals()
             on(widen, s + 4)
             on(outer_gpsimd, s)
+            on(outer_scalar, s, 1, 0, S_ROWS)
             on(logits, s + 1)
             on(read_values, s - 3)
             on(b_to_psum, s)
@@ -248,7 +245,9 @@ def tile_denseproductkeymemorygated_t_kernel(tc, x_bytes, x_scale, ka, kb, gs, v
             on(apply_gain, s - 2, 1)
             on(turn_w, s - 1, 1)
             on(outer_vector, s)
-            on(outer_scalar, s)
+            on(outer_scalar, s, 2, 0, NA)
             on(scale_x, s + 3)
+            on(sum_product, s + 1)
             on(finish, s - 3)
+            on(invert, s + 1)
             on(gate, s + 1)

@@ -22,28 +22,35 @@ R = NB // PACK
 G = 2
 IG = NA // G
 NT = T // P
-CH = 4
 KEYS = H * NA + H * NB
-S_ROWS, V_ROWS = 12, 6
+G_ROWS, V_ROWS = 48, 35
+FIRST = (40, 48)
+LAST = (40, 48)
+HEAD, TAIL = 0, 0
+NFIRST, NLAST = 1, 1
+PAIR = 2
+MERGE_V = 1
 
 
 def tile_denseproductkeymemorygated_t_kernel(tc, x_bytes, x_scale, ka, kb, gs, vals, wg, out):
     nc = tc.nc
+    groups = [(n, 1) for n in range(HEAD)] + [(n, PAIR) for n in range(HEAD, NT - TAIL, PAIR)] + [(n, 1) for n in range(NT - TAIL, NT)]
     with ExitStack() as ctx:
         keep = ctx.enter_context(tc.tile_pool(name="keep", bufs=1))
-        xin = ctx.enter_context(tc.tile_pool(name="xin", bufs=NT // CH))
+        xin = ctx.enter_context(tc.tile_pool(name="xin", bufs=len(groups)))
         work = ctx.enter_context(tc.tile_pool(name="work", bufs=3))
         gate_pool = ctx.enter_context(tc.tile_pool(name="gate", bufs=6))
+        prods = ctx.enter_context(tc.tile_pool(name="prods", bufs=3))
         ps1 = ctx.enter_context(tc.psum_pool(name="ps1", bufs=1))
-        ps2 = ctx.enter_context(tc.psum_pool(name="ps2", bufs=2))
-        ps3 = ctx.enter_context(tc.psum_pool(name="ps3", bufs=3))
+        ps4 = ctx.enter_context(tc.psum_pool(name="ps4", bufs=4))
         ctx.enter_context(tc.manual_schedule())
 
         xraw = {}
 
-        def load_x(c):
-            xraw[c] = xin.tile([P, CH, D], U8, name="xraw")
-            nc.sync.dma_start(out=xraw[c][:], in_=x_bytes[c * CH * P:(c + 1) * CH * P, :].rearrange("(p q) k -> p q k", q=CH))
+        def load_x(m):
+            n0, w = groups[m]
+            xraw[m] = xin.tile([P, w, D], U8, name="xraw")
+            nc.sync.dma_start(out=xraw[m][:], in_=x_bytes[n0 * P:(n0 + w) * P, :].rearrange("(p q) k -> p q k", q=w))
 
         load_x(0)
         xs = keep.tile([P, PACK], F32, name="xs")
@@ -52,14 +59,16 @@ def tile_denseproductkeymemorygated_t_kernel(tc, x_bytes, x_scale, ka, kb, gs, v
         nc.sync.dma_start(out=ka_raw[:], in_=ka.rearrange("(p t) h i -> p t (h i)", t=PACK))
         kb_raw = keep.tile([P, PACK, H * NB], BF16, name="kb_raw")
         nc.sync.dma_start(out=kb_raw[:], in_=kb.rearrange("(p t) h j -> p t (h j)", t=PACK))
+        load_x(1)
         wg_raw = keep.tile([P, PACK, V], BF16, name="wg_raw")
         nc.sync.dma_start(out=wg_raw[:], in_=wg.rearrange("(p t) v -> p t v", t=PACK))
+        load_x(2)
         vals_raw = keep.tile([P, G, PACK * V], BF16, name="vals_raw")
         nc.sync.dma_start(out=vals_raw[:], in_=vals.rearrange("i j v -> (i j) v").rearrange("(g p t) v -> p g (t v)", g=G, t=PACK))
         gain = keep.tile([P, G, PACK], BF16, name="gain")
         nc.sync.dma_start(out=gain[:], in_=gs.rearrange("i j -> (i j)").rearrange("(g p t) -> p g t", g=G, t=PACK))
-        for c in range(1, NT // CH):
-            load_x(c)
+        for m in range(3, len(groups)):
+            load_x(m)
 
         ident = keep.tile([P, P], F32, name="ident")
         make_identity(nc, ident[:])
@@ -70,12 +79,16 @@ def tile_denseproductkeymemorygated_t_kernel(tc, x_bytes, x_scale, ka, kb, gs, v
             out=w_grp[:, H * NA:KEYS, :].rearrange("p (h s r) t -> p h s r t", h=H, s=PACK),
             in_=kb_raw[:].rearrange("p t (h r s) -> p h s r t", h=H, s=PACK),
         )
-        nc.vector.tensor_copy(out=w_grp[:, KEYS:KEYS + V, :], in_=wg_raw[:].rearrange("p t c -> p c t"))
         w_codes = keep.tile([P, KEYS + V], U32, name="w_codes", align_bytes=64)
         w_scales = keep.tile([P, KEYS + V], U8, name="w_scales", align_bytes=64)
-        for lo, hi in ((0, KEYS), (KEYS, KEYS + V)):
+
+        def quantise_weights(lo, hi):
             nc.vector.quantize_mx(out=w_codes[:, lo:hi].bitcast(FP8X4), scales=w_scales[:, lo:hi],
                                   in_=w_grp[:, lo:hi, :].rearrange("p c t -> p (c t)"))
+
+        def group_gate_weights():
+            nc.vector.tensor_copy(out=w_grp[:, KEYS:KEYS + V, :], in_=wg_raw[:].rearrange("p t c -> p c t"))
+
         v_grp = keep.tile([P, G, V, PACK], BF16, name="v_grp", align_bytes=64)
         v_codes = keep.tile([P, G * V], U32, name="v_codes", align_bytes=64)
         v_scales = keep.tile([P, G * V], U8, name="v_scales", align_bytes=64)
@@ -85,169 +98,231 @@ def tile_denseproductkeymemorygated_t_kernel(tc, x_bytes, x_scale, ka, kb, gs, v
             nc.vector.quantize_mx(out=v_codes[:].bitcast(FP8X4), scales=v_scales[:],
                                   in_=v_grp[:].rearrange("p g v t -> p (g v t)"))
 
-        xw, xt, xb, xq, xqs, lg, nm, e, sm, th, gt, cc, rc, an, bps = ({} for unused in range(15))
-        prod, wt, ub, uq, uqs, rr, ot = ({} for unused in range(7))
+        xw, xt, xb, xq, xqs, lg, nm, ea, eb, sm, th, gt, cc, rc, an, bps = ({} for unused in range(16))
+        prod, wt, ub, uq, uqs, zr = ({} for unused in range(6))
 
-        def widen(n):
-            xw[n] = work.tile([P, D], BF16, name="xw")
-            nc.scalar.copy(out=xw[n][:], in_=xraw[n // CH][:, n % CH, :].bitcast(FP8))
+        def widen(m):
+            xw[m] = work.tile([P, groups[m][1], D], BF16, name="xw")
+            nc.scalar.copy(out=xw[m][:], in_=xraw[m][:].bitcast(FP8))
 
-        def turn_x(n):
-            xt[n] = ps1.tile([P, 2, P], F32, name="xt")
-            words = xw[n][:].bitcast(F32)
-            for u in range(2):
-                nc.tensor.transpose(xt[n][:, u, :], words[:, u:D // 2:2], ident[:])
+        def turn_x(m):
+            w = groups[m][1]
+            xt[m] = ps1.tile([P, 2, w * P], F32, name="xt")
+            for j in range(w):
+                words = xw[m][:, j, :].bitcast(F32)
+                for u in range(2):
+                    nc.tensor.transpose(xt[m][:, u, j * P:(j + 1) * P], words[:, u:D // 2:2], ident[:])
 
-        def scale_x(n):
-            xb[n] = work.tile([P, P, 2, 2], BF16, name="xb", align_bytes=64)
+        def scale_x(m):
+            shape = [P, groups[m][1] * P, 2, 2]
+            xb[m] = work.tile(shape, BF16, name="xb", align_bytes=64)
             nc.vector.tensor_tensor(
-                out=xb[n][:],
-                in0=xt[n][:].rearrange("p u k -> p (u k)").bitcast(BF16).rearrange("p (u k e) -> p k u e", u=2, e=2),
-                in1=xs[:].rearrange("p (u e) -> p u e", u=2).unsqueeze(1).to_broadcast([P, P, 2, 2]),
+                out=xb[m][:],
+                in0=xt[m][:].rearrange("p u k -> p (u k)").bitcast(BF16).rearrange("p (u k e) -> p k u e", u=2, e=2),
+                in1=xs[:].rearrange("p (u e) -> p u e", u=2).unsqueeze(1).to_broadcast(shape),
                 op=ALU.mult)
 
-        def quantise_x(n):
-            xq[n] = work.tile([P, P], U32, name="xq", align_bytes=64)
-            xqs[n] = work.tile([P, P], U8, name="xqs", align_bytes=64)
-            nc.vector.quantize_mx(out=xq[n][:].bitcast(FP8X4), scales=xqs[n][:],
-                                  in_=xb[n][:].rearrange("p k u e -> p (k u e)"))
+        def quantise_x(m):
+            w = groups[m][1]
+            xq[m] = work.tile([P, w * P], U32, name="xq", align_bytes=64)
+            xqs[m] = work.tile([P, w * P], U8, name="xqs", align_bytes=64)
+            nc.vector.quantize_mx(out=xq[m][:].bitcast(FP8X4), scales=xqs[m][:],
+                                  in_=xb[m][:].rearrange("p k u e -> p (k u e)"))
 
-        def logits(n):
-            lg[n] = ps2.tile([P, KEYS + V], F32, name="lg")
-            for lo, hi in ((0, KEYS), (KEYS, KEYS + V)):
-                nc.tensor.matmul_mx(out=lg[n][:, lo:hi], lhsT=xq[n][:].bitcast(FP8X4), lhsT_scale=xqs[n][:],
-                                    rhs=w_codes[:, lo:hi].bitcast(FP8X4), rhs_scale=w_scales[:, lo:hi],
-                                    start=True, stop=True)
+        def step_bank(s):
+            if s not in zr:
+                zr[s] = ps1.tile([P, 2, PAIR, V], F32, name="zr")
+            return zr[s]
 
-        def row_max(n):
-            nm[n] = work.tile([P, 2 * H], F32, name="nm")
-            nc.vector.tensor_reduce(out=nm[n][:], in_=lg[n][:, 0:KEYS].rearrange("p (h i) -> p h i", i=NA),
+        def z_of(m):
+            return step_bank(m - 1)[:, 0, 0:groups[m][1], :]
+
+        def r_of(m):
+            return step_bank(m + 3)[:, 1, 0:groups[m][1], :]
+
+        def logits(m):
+            w = groups[m][1]
+            lg[m] = ps1.tile([P, w, KEYS], F32, name="lg")
+            for target, lo, hi in ((lg[m], 0, KEYS), (z_of(m), KEYS, KEYS + V)):
+                for j in range(w):
+                    tok = slice(j * P, (j + 1) * P)
+                    nc.tensor.matmul_mx(out=target[:, j, :], lhsT=xq[m][:, tok].bitcast(FP8X4), lhsT_scale=xqs[m][:, tok],
+                                        rhs=w_codes[:, lo:hi].bitcast(FP8X4), rhs_scale=w_scales[:, lo:hi],
+                                        start=True, stop=True)
+
+        def row_max(m):
+            nm[m] = work.tile([P, groups[m][1] * 2 * H], F32, name="nm")
+            nc.vector.tensor_reduce(out=nm[m][:], in_=lg[m][:].rearrange("p w (h i) -> p (w h) i", i=NA),
                                     axis=AX.X, op=ALU.max, negate=True)
 
-        def exps(n):
-            e[n] = work.tile([P, KEYS], F32, name="e")
-            sm[n] = work.tile([P, 2 * H], F32, name="sm")
-            for h in range(2 * H):
-                cols = slice(h * NA, (h + 1) * NA)
-                nc.scalar.activation(out=e[n][:, cols], in_=lg[n][:, cols], func=ACT.Exp, bias=nm[n][:, h:h + 1],
-                                     accum_out=sm[n][:, h:h + 1])
-            th[n] = work.tile([P, V], F32, name="th")
-            nc.scalar.activation(out=th[n][:], in_=lg[n][:, KEYS:KEYS + V], func=ACT.Tanh, scale=0.5)
+        def exps(m):
+            w = groups[m][1]
+            ea[m] = work.tile([P, H, w, NA], F32, name="ea")
+            eb[m] = work.tile([P, H, PACK, w, R], F32, name="eb")
+            sm[m] = work.tile([P, 2, H, w], F32, name="sm")
+            for j in range(w):
+                for h in range(H):
+                    for u, target in enumerate((ea[m][:, h, j, :].rearrange("p (t r) -> p t r", r=R), eb[m][:, h, :, j, :])):
+                        c = u * H + h
+                        nc.scalar.activation(out=target, in_=lg[m][:, j, c * NA:(c + 1) * NA].rearrange("p (t r) -> p t r", r=R),
+                                             func=ACT.Exp, bias=nm[m][:, j * 2 * H + c:j * 2 * H + c + 1],
+                                             accum_out=sm[m][:, u, h, j:j + 1])
 
-        def gate(n):
-            gt[n] = gate_pool.tile([P, V], F32, name="gt")
-            nc.vector.scalar_tensor_tensor(out=gt[n][:], in0=th[n][:], scalar=1.0, in1=lg[n][:, KEYS:KEYS + V],
-                                           op0=ALU.add, op1=ALU.mult)
+        def half_tanh(m):
+            th[m] = work.tile([P, groups[m][1], V], F32, name="th")
+            nc.scalar.activation(out=th[m][:], in_=z_of(m), func=ACT.Tanh, scale=0.5)
 
-        def sum_product(n):
-            cc[n] = work.tile([P, H], F32, name="cc")
-            nc.vector.tensor_reduce(out=cc[n][:], in_=sm[n][:].rearrange("p (u h) -> p h u", u=2), axis=AX.X, op=ALU.mult)
+        def gate(m):
+            gt[m] = gate_pool.tile([P, groups[m][1], V], F32, name="gt")
+            nc.vector.scalar_tensor_tensor(out=gt[m][:], in0=th[m][:], scalar=1.0, in1=z_of(m), op0=ALU.add, op1=ALU.mult)
 
-        def invert(n):
-            rc[n] = work.tile([P, H], F32, name="rc")
-            nc.vector.reciprocal(out=rc[n][:], in_=cc[n][:])
+        def sum_product(m):
+            cc[m] = work.tile([P, H * groups[m][1]], F32, name="cc")
+            nc.vector.tensor_reduce(out=cc[m][:], in_=sm[m][:].rearrange("p u h w -> p (h w) u"), axis=AX.X, op=ALU.mult)
 
-        def normalise(n):
-            an[n] = work.tile([P, H, NA], F32, name="an")
-            nc.vector.tensor_tensor(out=an[n][:], in0=e[n][:, 0:H * NA].rearrange("p (h i) -> p h i", h=H),
-                                    in1=rc[n][:].unsqueeze(2).to_broadcast([P, H, NA]), op=ALU.mult)
+        def invert(m):
+            rc[m] = work.tile([P, H * groups[m][1]], F32, name="rc")
+            nc.vector.reciprocal(out=rc[m][:], in_=cc[m][:])
 
-        def b_to_psum(n):
-            bps[n] = ps1.tile([P, H * NB], F32, name="bps")
-            nc.tensor.matmul(out=bps[n][:], lhsT=ident[:], rhs=e[n][:, H * NA:KEYS], start=True, stop=True)
+        def normalise(m):
+            w = groups[m][1]
+            an[m] = work.tile([P, H, w, NA], F32, name="an")
+            nc.vector.tensor_tensor(out=an[m][:].rearrange("p h w i -> p (h w) i"), in0=ea[m][:].rearrange("p h w i -> p (h w) i"),
+                                    in1=rc[m][:].unsqueeze(2).to_broadcast([P, H * w, NA]), op=ALU.mult)
 
-        def head_tile(n, h):
-            if (n, h) not in prod:
-                prod[n, h] = work.tile([P, PACK, NA, R], F32, name="prod%d" % h)
-            return prod[n, h]
+        def b_to_psum(m):
+            bps[m] = ps1.tile([P, 2, PACK, groups[m][1], R], F32, name="bps")
+            nc.tensor.matmul(out=bps[m][:].rearrange("p h t w r -> p (h t w r)"), lhsT=ident[:],
+                             rhs=eb[m][:, 0:2, :, :, :].rearrange("p h t w r -> p (h t w r)"), start=True, stop=True)
 
-        def b_of(n, h):
-            return e[n][:, H * NA + h * NB:H * NA + (h + 1) * NB]
+        def head_tile(m, h):
+            if (m, h) not in prod:
+                prod[m, h] = prods.tile([P, PACK, groups[m][1], NA, R], F32, name="prod%d" % h)
+            return prod[m, h]
 
-        def outer(engine, n, h, b_cols, i0, i1):
-            shape = [P, PACK, i1 - i0, R]
+        def row_split(m, j):
+            w = groups[m][1]
+            g_rows, v_rows = FIRST if m < NFIRST else LAST if m >= len(groups) - NLAST else (G_ROWS, V_ROWS)
+            return NA + ((v_rows - NA) * w if j == 0 else 0), (H - 1) * NA - ((g_rows - NA) * w if j == w - 1 else 0)
+
+        def outer_rows(engine, m, j, h, b, i0, i1):
+            if i1 > i0:
+                shape = [P, PACK, i1 - i0, R]
+                engine.tensor_tensor(
+                    out=head_tile(m, h)[:, :, j, i0:i1, :],
+                    in0=b[:, h, :, j, :].unsqueeze(2).to_broadcast(shape),
+                    in1=an[m][:, h, j, i0:i1].unsqueeze(1).unsqueeze(3).to_broadcast(shape),
+                    op=ALU.mult)
+
+        def outer_head(engine, m, h, b):
+            w = groups[m][1]
             engine.tensor_tensor(
-                out=head_tile(n, h)[:, :, i0:i1, :],
-                in0=b_cols.rearrange("p (t r) -> p t r", r=R).unsqueeze(2).to_broadcast(shape),
-                in1=an[n][:, h, i0:i1].unsqueeze(1).unsqueeze(3).to_broadcast(shape),
+                out=head_tile(m, h)[:].rearrange("p t w i r -> p (t w i r)"),
+                in0=b[:, h, :, :, :].rearrange("p t w r -> p (t w) r").unsqueeze(2).to_broadcast([P, PACK * w, NA, R]),
+                in1=an[m][:, h, :, :].rearrange("p w i -> p (w i)").unsqueeze(1).unsqueeze(3).to_broadcast([P, PACK, w * NA, R]),
                 op=ALU.mult)
 
-        def outer_gpsimd(n):
-            outer(nc.gpsimd, n, 3, b_of(n, 3), 0, NA)
-            outer(nc.gpsimd, n, 1, b_of(n, 1), S_ROWS + V_ROWS, NA)
+        def outer_gpsimd(m):
+            w = groups[m][1]
+            outer_head(nc.gpsimd, m, 3, eb[m])
+            outer_rows(nc.gpsimd, m, w - 1, 2, eb[m], row_split(m, w - 1)[1] - 2 * NA, NA)
 
-        def outer_vector(n):
-            outer(nc.vector, n, 0, bps[n][:, 0:NB], 0, NA)
-            outer(nc.vector, n, 1, bps[n][:, NB:2 * NB], S_ROWS, S_ROWS + V_ROWS)
+        def outer_vector(m, j):
+            if MERGE_V:
+                if j == 0:
+                    outer_head(nc.vector, m, 0, bps[m])
+            elif j < groups[m][1]:
+                outer_rows(nc.vector, m, j, 0, bps[m], 0, NA)
 
-        def outer_scalar(n, h, i0, i1):
-            for i in range(i0, i1):
-                nc.scalar.activation(out=head_tile(n, h)[:, :, i, :], in_=b_of(n, h).rearrange("p (t r) -> p t r", r=R),
-                                     func=ACT.Copy, scale=an[n][:, h, i:i + 1])
+        def outer_vector_shared(m):
+            outer_rows(nc.vector, m, 0, 1, bps[m], 0, row_split(m, 0)[0] - NA)
 
-        def turn_w(n, g):
-            wt[n, g] = ps3.tile([P, PACK, P], F32, name="wt")
-            for t in range(PACK):
-                for h in range(H):
-                    nc.tensor.matmul(out=wt[n, g][:, t, :], lhsT=prod[n, h][:, t, g * IG:(g + 1) * IG, :].rearrange("p i r -> p (i r)"), rhs=ident[:],
-                                     is_transpose=True, start=(h == 0), stop=(h == H - 1))
+        def outer_scalar(m, j, h):
+            if j < groups[m][1]:
+                lo, hi = row_split(m, j)
+                for i in range(max(lo - h * NA, 0), min(hi - h * NA, NA)):
+                    nc.scalar.activation(out=head_tile(m, h)[:, :, j, i, :], in_=eb[m][:, h, :, j, :],
+                                         func=ACT.Copy, scale=an[m][:, h, j, i:i + 1])
 
-        def apply_gain(n, g):
-            if g == 0:
-                ub[n] = work.tile([P, G, P, PACK], BF16, name="ub", align_bytes=64)
-            nc.vector.tensor_tensor(out=ub[n][:, g, :, :], in0=wt[n, g][:].rearrange("p t k -> p k t"),
-                                    in1=gain[:, g, :].unsqueeze(1).to_broadcast([P, P, PACK]), op=ALU.mult)
+        def turn_w(m, j, g):
+            if j < groups[m][1]:
+                wt[m, j, g] = ps4.tile([P, PACK, P], F32, name="wt")
+                for t in range(PACK):
+                    for h in range(H):
+                        nc.tensor.matmul(out=wt[m, j, g][:, t, :],
+                                         lhsT=prod[m, h][:, t, j, g * IG:(g + 1) * IG, :].rearrange("p i r -> p (i r)"),
+                                         rhs=ident[:], is_transpose=True, start=(h == 0), stop=(h == H - 1))
 
-        def quantise_u(n):
-            uq[n] = work.tile([P, G * P], U32, name="uq", align_bytes=64)
-            uqs[n] = work.tile([P, G * P], U8, name="uqs", align_bytes=64)
-            nc.vector.quantize_mx(out=uq[n][:].bitcast(FP8X4), scales=uqs[n][:],
-                                  in_=ub[n][:].rearrange("p g k t -> p (g k t)"))
+        def apply_gain(m, j, g):
+            w = groups[m][1]
+            if j < w:
+                if m not in ub:
+                    ub[m] = work.tile([P, w, G, P, PACK], BF16, name="ub", align_bytes=64)
+                nc.vector.tensor_tensor(out=ub[m][:, j, g, :, :], in0=wt[m, j, g][:].rearrange("p t k -> p k t"),
+                                        in1=gain[:, g, :].unsqueeze(1).to_broadcast([P, P, PACK]), op=ALU.mult)
 
-        def read_values(n):
-            rr[n] = ps1.tile([P, V], F32, name="rr")
-            for g in range(G):
-                nc.tensor.matmul_mx(out=rr[n][:], lhsT=uq[n][:, g * P:(g + 1) * P].bitcast(FP8X4),
-                                    lhsT_scale=uqs[n][:, g * P:(g + 1) * P],
-                                    rhs=v_codes[:, g * V:(g + 1) * V].bitcast(FP8X4), rhs_scale=v_scales[:, g * V:(g + 1) * V],
-                                    start=(g == 0), stop=(g == G - 1))
+        def quantise_u(m):
+            w = groups[m][1]
+            uq[m] = work.tile([P, w * G * P], U32, name="uq", align_bytes=64)
+            uqs[m] = work.tile([P, w * G * P], U8, name="uqs", align_bytes=64)
+            nc.vector.quantize_mx(out=uq[m][:].bitcast(FP8X4), scales=uqs[m][:],
+                                  in_=ub[m][:].rearrange("p w g k t -> p (w g k t)"))
 
-        def finish(n):
-            c, q = divmod(n, CH)
-            if q == 0:
-                ot[c] = work.tile([P, CH, V], F32, name="ot")
-            nc.vector.scalar_tensor_tensor(out=ot[c][:, q, :], in0=rr[n][:], scalar=0.5, in1=gt[n][:],
-                                           op0=ALU.mult, op1=ALU.mult)
-            if q == CH - 1:
-                nc.sync.dma_start(out=out[c * CH * P:(c + 1) * CH * P, :].rearrange("(p q) v -> p q v", q=CH), in_=ot[c][:])
+        def read_values(m):
+            for j in range(groups[m][1]):
+                for g in range(G):
+                    tok = slice((j * G + g) * P, (j * G + g + 1) * P)
+                    nc.tensor.matmul_mx(out=r_of(m)[:, j, :], lhsT=uq[m][:, tok].bitcast(FP8X4), lhsT_scale=uqs[m][:, tok],
+                                        rhs=v_codes[:, g * V:(g + 1) * V].bitcast(FP8X4), rhs_scale=v_scales[:, g * V:(g + 1) * V],
+                                        start=(g == 0), stop=(g == G - 1))
 
-        def on(stage, n, *more):
-            if 0 <= n < NT:
-                stage(n, *more)
+        def finish(m):
+            n0, w = groups[m]
+            ot = work.tile([P, w, V], F32, name="ot")
+            nc.vector.scalar_tensor_tensor(out=ot[:], in0=r_of(m), scalar=0.5, in1=gt[m][:], op0=ALU.mult, op1=ALU.mult)
+            nc.sync.dma_start(out=out[n0 * P:(n0 + w) * P, :].rearrange("(p q) v -> p q v", q=w), in_=ot[:])
 
-        for s in range(-4, NT + 3):
-            on(quantise_u, s - 3)
-            on(quantise_x, s + 2)
-            on(normalise, s)
-            if s == 0:
+        def on(stage, m, *more):
+            if 0 <= m < len(groups):
+                stage(m, *more)
+
+        for s in range(-3, len(groups) + 3):
+            on(quantise_x, s + 1)
+            if s == -1:
+                quantise_weights(KEYS, KEYS + V)
+            on(quantise_u, s - 2)
+            if s == 1:
                 quantise_vals()
-            on(widen, s + 4)
+            on(normalise, s)
             on(outer_gpsimd, s)
-            on(outer_scalar, s, 1, 0, S_ROWS)
+            on(turn_x, s + 2)
             on(logits, s + 1)
             on(read_values, s - 3)
             on(b_to_psum, s)
-            on(turn_x, s + 3)
+            on(turn_w, s - 1, 1, 0)
+            on(turn_w, s - 1, 1, 1)
+            on(widen, s + 3)
+            on(half_tanh, s + 1)
+            on(outer_scalar, s, 0, 1)
+            on(outer_scalar, s, 0, 2)
+            on(apply_gain, s - 1, 0, 0)
+            on(apply_gain, s - 1, 0, 1)
             on(row_max, s + 1)
             on(exps, s + 1)
-            on(apply_gain, s - 2, 0)
-            on(turn_w, s - 1, 0)
-            on(apply_gain, s - 2, 1)
-            on(turn_w, s - 1, 1)
-            on(outer_vector, s)
-            on(outer_scalar, s, 2, 0, NA)
-            on(scale_x, s + 3)
-            on(sum_product, s + 1)
+            on(outer_scalar, s, 1, 1)
+            on(outer_scalar, s, 1, 2)
+            on(outer_vector, s, 0)
+            on(outer_vector_shared, s)
+            on(turn_w, s, 0, 0)
+            on(turn_w, s, 0, 1)
+            on(scale_x, s + 2)
+            if s == -2:
+                quantise_weights(0, KEYS)
+                group_gate_weights()
             on(finish, s - 3)
-            on(invert, s + 1)
+            on(apply_gain, s - 1, 1, 0)
+            on(apply_gain, s - 1, 1, 1)
+            on(outer_vector, s, 1)
+            on(sum_product, s + 1)
             on(gate, s + 1)
+            on(invert, s + 1)

@@ -19,38 +19,35 @@ AX = mybir.AxisListType
 P = 128
 PACK = 4
 R = NB // PACK
-G = 2
+G = NA * NB // (P * PACK)
 IG = NA // G
-NT = T // P
+W = 2
+PAIRS = T // (W * P)
 KEYS = H * NA + H * NB
-G_ROWS, V_ROWS = 48, 35
-FIRST = (40, 48)
-LAST = (40, 48)
-HEAD, TAIL = 0, 0
-NFIRST, NLAST = 1, 1
-PAIR = 2
-MERGE_V = 1
+
+VECTOR_ROWS = 6
 
 
 def tile_denseproductkeymemorygated_t_kernel(tc, x_bytes, x_scale, ka, kb, gs, vals, wg, out):
     nc = tc.nc
-    groups = [(n, 1) for n in range(HEAD)] + [(n, PAIR) for n in range(HEAD, NT - TAIL, PAIR)] + [(n, 1) for n in range(NT - TAIL, NT)]
     with ExitStack() as ctx:
         keep = ctx.enter_context(tc.tile_pool(name="keep", bufs=1))
-        xin = ctx.enter_context(tc.tile_pool(name="xin", bufs=len(groups)))
+        xin = ctx.enter_context(tc.tile_pool(name="xin", bufs=PAIRS))
         work = ctx.enter_context(tc.tile_pool(name="work", bufs=3))
-        gate_pool = ctx.enter_context(tc.tile_pool(name="gate", bufs=6))
         prods = ctx.enter_context(tc.tile_pool(name="prods", bufs=3))
+        gates = ctx.enter_context(tc.tile_pool(name="gates", bufs=6))
         ps1 = ctx.enter_context(tc.psum_pool(name="ps1", bufs=1))
-        ps4 = ctx.enter_context(tc.psum_pool(name="ps4", bufs=4))
+        ps4 = ctx.enter_context(tc.psum_pool(name="ps4", bufs=W * G))
         ctx.enter_context(tc.manual_schedule())
+
+        def tokens_of(dram, m):
+            return dram[m * W * P:(m + 1) * W * P, :].rearrange("(p w) c -> p w c", w=W)
 
         xraw = {}
 
         def load_x(m):
-            n0, w = groups[m]
-            xraw[m] = xin.tile([P, w, D], U8, name="xraw")
-            nc.sync.dma_start(out=xraw[m][:], in_=x_bytes[n0 * P:(n0 + w) * P, :].rearrange("(p q) k -> p q k", q=w))
+            xraw[m] = xin.tile([P, W, D], U8, name="xraw")
+            nc.sync.dma_start(out=xraw[m][:], in_=tokens_of(x_bytes, m))
 
         load_x(0)
         xs = keep.tile([P, PACK], F32, name="xs")
@@ -64,30 +61,31 @@ def tile_denseproductkeymemorygated_t_kernel(tc, x_bytes, x_scale, ka, kb, gs, v
         nc.sync.dma_start(out=wg_raw[:], in_=wg.rearrange("(p t) v -> p t v", t=PACK))
         load_x(2)
         vals_raw = keep.tile([P, G, PACK * V], BF16, name="vals_raw")
-        nc.sync.dma_start(out=vals_raw[:], in_=vals.rearrange("i j v -> (i j) v").rearrange("(g p t) v -> p g (t v)", g=G, t=PACK))
+        nc.sync.dma_start(out=vals_raw[:],
+                          in_=vals.rearrange("i j v -> (i j) v").rearrange("(g p t) v -> p g (t v)", g=G, t=PACK))
         gain = keep.tile([P, G, PACK], BF16, name="gain")
         nc.sync.dma_start(out=gain[:], in_=gs.rearrange("i j -> (i j)").rearrange("(g p t) -> p g t", g=G, t=PACK))
-        for m in range(3, len(groups)):
+        for m in range(3, PAIRS):
             load_x(m)
 
         ident = keep.tile([P, P], F32, name="ident")
         make_identity(nc, ident[:])
 
         w_grp = keep.tile([P, KEYS + V, PACK], BF16, name="w_grp", align_bytes=64)
+        w_codes = keep.tile([P, KEYS + V], U32, name="w_codes", align_bytes=64)
+        w_scales = keep.tile([P, KEYS + V], U8, name="w_scales", align_bytes=64)
         nc.vector.tensor_copy(out=w_grp[:, 0:H * NA, :], in_=ka_raw[:].rearrange("p t c -> p c t"))
         nc.vector.tensor_copy(
             out=w_grp[:, H * NA:KEYS, :].rearrange("p (h s r) t -> p h s r t", h=H, s=PACK),
             in_=kb_raw[:].rearrange("p t (h r s) -> p h s r t", h=H, s=PACK),
         )
-        w_codes = keep.tile([P, KEYS + V], U32, name="w_codes", align_bytes=64)
-        w_scales = keep.tile([P, KEYS + V], U8, name="w_scales", align_bytes=64)
+
+        def group_gate_weights():
+            nc.vector.tensor_copy(out=w_grp[:, KEYS:KEYS + V, :], in_=wg_raw[:].rearrange("p t c -> p c t"))
 
         def quantise_weights(lo, hi):
             nc.vector.quantize_mx(out=w_codes[:, lo:hi].bitcast(FP8X4), scales=w_scales[:, lo:hi],
                                   in_=w_grp[:, lo:hi, :].rearrange("p c t -> p (c t)"))
-
-        def group_gate_weights():
-            nc.vector.tensor_copy(out=w_grp[:, KEYS:KEYS + V, :], in_=wg_raw[:].rearrange("p t c -> p c t"))
 
         v_grp = keep.tile([P, G, V, PACK], BF16, name="v_grp", align_bytes=64)
         v_codes = keep.tile([P, G * V], U32, name="v_codes", align_bytes=64)
@@ -98,195 +96,182 @@ def tile_denseproductkeymemorygated_t_kernel(tc, x_bytes, x_scale, ka, kb, gs, v
             nc.vector.quantize_mx(out=v_codes[:].bitcast(FP8X4), scales=v_scales[:],
                                   in_=v_grp[:].rearrange("p g v t -> p (g v t)"))
 
-        xw, xt, xb, xq, xqs, lg, nm, ea, eb, sm, th, gt, cc, rc, an, bps = ({} for unused in range(16))
-        prod, wt, ub, uq, uqs, zr = ({} for unused in range(6))
+        x_wide, x_turned, x_bf, x_codes, x_scales = {}, {}, {}, {}, {}
+        logit, neg_max, exp_a, exp_b, sums, sum_prod, inv, a_norm, b_psum = {}, {}, {}, {}, {}, {}, {}, {}, {}
+        half_tanh, gate, zr_bank = {}, {}, {}
+        prod, w_turned, u_bf, u_codes, u_scales = {}, {}, {}, {}, {}
 
-        def widen(m):
-            xw[m] = work.tile([P, groups[m][1], D], BF16, name="xw")
-            nc.scalar.copy(out=xw[m][:], in_=xraw[m][:].bitcast(FP8))
+        def widen_x(m):
+            x_wide[m] = work.tile([P, W, D], BF16, name="x_wide")
+            nc.scalar.copy(out=x_wide[m][:], in_=xraw[m][:].bitcast(FP8))
 
         def turn_x(m):
-            w = groups[m][1]
-            xt[m] = ps1.tile([P, 2, w * P], F32, name="xt")
-            for j in range(w):
-                words = xw[m][:, j, :].bitcast(F32)
+            x_turned[m] = ps1.tile([P, 2, W * P], F32, name="x_turned")
+            for j in range(W):
+                words = x_wide[m][:, j, :].bitcast(F32)
                 for u in range(2):
-                    nc.tensor.transpose(xt[m][:, u, j * P:(j + 1) * P], words[:, u:D // 2:2], ident[:])
+                    nc.tensor.transpose(x_turned[m][:, u, j * P:(j + 1) * P], words[:, u:D // 2:2], ident[:])
 
         def scale_x(m):
-            shape = [P, groups[m][1] * P, 2, 2]
-            xb[m] = work.tile(shape, BF16, name="xb", align_bytes=64)
+            shape = [P, W * P, 2, 2]
+            x_bf[m] = work.tile(shape, BF16, name="x_bf", align_bytes=64)
             nc.vector.tensor_tensor(
-                out=xb[m][:],
-                in0=xt[m][:].rearrange("p u k -> p (u k)").bitcast(BF16).rearrange("p (u k e) -> p k u e", u=2, e=2),
+                out=x_bf[m][:],
+                in0=x_turned[m][:].rearrange("p u n -> p (u n)").bitcast(BF16).rearrange("p (u n e) -> p n u e", u=2, e=2),
                 in1=xs[:].rearrange("p (u e) -> p u e", u=2).unsqueeze(1).to_broadcast(shape),
                 op=ALU.mult)
 
         def quantise_x(m):
-            w = groups[m][1]
-            xq[m] = work.tile([P, w * P], U32, name="xq", align_bytes=64)
-            xqs[m] = work.tile([P, w * P], U8, name="xqs", align_bytes=64)
-            nc.vector.quantize_mx(out=xq[m][:].bitcast(FP8X4), scales=xqs[m][:],
-                                  in_=xb[m][:].rearrange("p k u e -> p (k u e)"))
+            x_codes[m] = work.tile([P, W * P], U32, name="x_codes", align_bytes=64)
+            x_scales[m] = work.tile([P, W * P], U8, name="x_scales", align_bytes=64)
+            nc.vector.quantize_mx(out=x_codes[m][:].bitcast(FP8X4), scales=x_scales[m][:],
+                                  in_=x_bf[m][:].rearrange("p n u e -> p (n u e)"))
 
-        def step_bank(s):
-            if s not in zr:
-                zr[s] = ps1.tile([P, 2, PAIR, V], F32, name="zr")
-            return zr[s]
+        def bank_of_step(s):
+            if s not in zr_bank:
+                zr_bank[s] = ps1.tile([P, 2, W, V], F32, name="zr_bank")
+            return zr_bank[s]
 
         def z_of(m):
-            return step_bank(m - 1)[:, 0, 0:groups[m][1], :]
+            return bank_of_step(m - 1)[:, 0, :, :]
 
         def r_of(m):
-            return step_bank(m + 3)[:, 1, 0:groups[m][1], :]
+            return bank_of_step(m + 3)[:, 1, :, :]
 
-        def logits(m):
-            w = groups[m][1]
-            lg[m] = ps1.tile([P, w, KEYS], F32, name="lg")
-            for target, lo, hi in ((lg[m], 0, KEYS), (z_of(m), KEYS, KEYS + V)):
-                for j in range(w):
+        def project(m):
+            logit[m] = ps1.tile([P, W, KEYS], F32, name="logit")
+            for target, lo, hi in ((logit[m], 0, KEYS), (z_of(m), KEYS, KEYS + V)):
+                for j in range(W):
                     tok = slice(j * P, (j + 1) * P)
-                    nc.tensor.matmul_mx(out=target[:, j, :], lhsT=xq[m][:, tok].bitcast(FP8X4), lhsT_scale=xqs[m][:, tok],
-                                        rhs=w_codes[:, lo:hi].bitcast(FP8X4), rhs_scale=w_scales[:, lo:hi],
-                                        start=True, stop=True)
+                    nc.tensor.matmul_mx(out=target[:, j, :], lhsT=x_codes[m][:, tok].bitcast(FP8X4),
+                                        lhsT_scale=x_scales[m][:, tok], rhs=w_codes[:, lo:hi].bitcast(FP8X4),
+                                        rhs_scale=w_scales[:, lo:hi], start=True, stop=True)
 
         def row_max(m):
-            nm[m] = work.tile([P, groups[m][1] * 2 * H], F32, name="nm")
-            nc.vector.tensor_reduce(out=nm[m][:], in_=lg[m][:].rearrange("p w (h i) -> p (w h) i", i=NA),
+            neg_max[m] = work.tile([P, W * 2 * H], F32, name="neg_max")
+            nc.vector.tensor_reduce(out=neg_max[m][:], in_=logit[m][:].rearrange("p w (c i) -> p (w c) i", i=NA),
                                     axis=AX.X, op=ALU.max, negate=True)
 
         def exps(m):
-            w = groups[m][1]
-            ea[m] = work.tile([P, H, w, NA], F32, name="ea")
-            eb[m] = work.tile([P, H, PACK, w, R], F32, name="eb")
-            sm[m] = work.tile([P, 2, H, w], F32, name="sm")
-            for j in range(w):
+            exp_a[m] = work.tile([P, H, W, NA], F32, name="exp_a")
+            exp_b[m] = work.tile([P, H, PACK, W, R], F32, name="exp_b")
+            sums[m] = work.tile([P, 2, H, W], F32, name="sums")
+            for j in range(W):
                 for h in range(H):
-                    for u, target in enumerate((ea[m][:, h, j, :].rearrange("p (t r) -> p t r", r=R), eb[m][:, h, :, j, :])):
-                        c = u * H + h
-                        nc.scalar.activation(out=target, in_=lg[m][:, j, c * NA:(c + 1) * NA].rearrange("p (t r) -> p t r", r=R),
-                                             func=ACT.Exp, bias=nm[m][:, j * 2 * H + c:j * 2 * H + c + 1],
-                                             accum_out=sm[m][:, u, h, j:j + 1])
+                    targets = (exp_a[m][:, h, j, :].rearrange("p (t r) -> p t r", r=R), exp_b[m][:, h, :, j, :])
+                    for half, target in enumerate(targets):
+                        c = half * H + h
+                        nc.scalar.activation(
+                            out=target, in_=logit[m][:, j, c * NA:(c + 1) * NA].rearrange("p (t r) -> p t r", r=R),
+                            func=ACT.Exp, bias=neg_max[m][:, j * 2 * H + c:j * 2 * H + c + 1],
+                            accum_out=sums[m][:, half, h, j:j + 1])
 
-        def half_tanh(m):
-            th[m] = work.tile([P, groups[m][1], V], F32, name="th")
-            nc.scalar.activation(out=th[m][:], in_=z_of(m), func=ACT.Tanh, scale=0.5)
+        def tanh_z(m):
+            half_tanh[m] = work.tile([P, W, V], F32, name="half_tanh")
+            nc.scalar.activation(out=half_tanh[m][:], in_=z_of(m), func=ACT.Tanh, scale=0.5)
 
-        def gate(m):
-            gt[m] = gate_pool.tile([P, groups[m][1], V], F32, name="gt")
-            nc.vector.scalar_tensor_tensor(out=gt[m][:], in0=th[m][:], scalar=1.0, in1=z_of(m), op0=ALU.add, op1=ALU.mult)
+        def make_gate(m):
+            gate[m] = gates.tile([P, W, V], F32, name="gate")
+            nc.vector.scalar_tensor_tensor(out=gate[m][:], in0=half_tanh[m][:], scalar=1.0, in1=z_of(m),
+                                           op0=ALU.add, op1=ALU.mult)
 
-        def sum_product(m):
-            cc[m] = work.tile([P, H * groups[m][1]], F32, name="cc")
-            nc.vector.tensor_reduce(out=cc[m][:], in_=sm[m][:].rearrange("p u h w -> p (h w) u"), axis=AX.X, op=ALU.mult)
+        def multiply_sums(m):
+            sum_prod[m] = work.tile([P, H * W], F32, name="sum_prod")
+            nc.vector.tensor_reduce(out=sum_prod[m][:], in_=sums[m][:].rearrange("p u h w -> p (h w) u"),
+                                    axis=AX.X, op=ALU.mult)
 
         def invert(m):
-            rc[m] = work.tile([P, H * groups[m][1]], F32, name="rc")
-            nc.vector.reciprocal(out=rc[m][:], in_=cc[m][:])
+            inv[m] = work.tile([P, H * W], F32, name="inv")
+            nc.vector.reciprocal(out=inv[m][:], in_=sum_prod[m][:])
 
         def normalise(m):
-            w = groups[m][1]
-            an[m] = work.tile([P, H, w, NA], F32, name="an")
-            nc.vector.tensor_tensor(out=an[m][:].rearrange("p h w i -> p (h w) i"), in0=ea[m][:].rearrange("p h w i -> p (h w) i"),
-                                    in1=rc[m][:].unsqueeze(2).to_broadcast([P, H * w, NA]), op=ALU.mult)
+            a_norm[m] = work.tile([P, H, W, NA], F32, name="a_norm")
+            nc.vector.tensor_tensor(out=a_norm[m][:].rearrange("p h w i -> p (h w) i"),
+                                    in0=exp_a[m][:].rearrange("p h w i -> p (h w) i"),
+                                    in1=inv[m][:].unsqueeze(2).to_broadcast([P, H * W, NA]), op=ALU.mult)
 
         def b_to_psum(m):
-            bps[m] = ps1.tile([P, 2, PACK, groups[m][1], R], F32, name="bps")
-            nc.tensor.matmul(out=bps[m][:].rearrange("p h t w r -> p (h t w r)"), lhsT=ident[:],
-                             rhs=eb[m][:, 0:2, :, :, :].rearrange("p h t w r -> p (h t w r)"), start=True, stop=True)
+            b_psum[m] = ps1.tile([P, H, PACK, W, R], F32, name="b_psum")
+            nc.tensor.matmul(out=b_psum[m][:].rearrange("p h t w r -> p (h t w r)"), lhsT=ident[:],
+                             rhs=exp_b[m][:].rearrange("p h t w r -> p (h t w r)"), start=True, stop=True)
 
         def head_tile(m, h):
             if (m, h) not in prod:
-                prod[m, h] = prods.tile([P, PACK, groups[m][1], NA, R], F32, name="prod%d" % h)
+                prod[m, h] = prods.tile([P, PACK, W, NA, R], F32, name="prod%d" % h)
             return prod[m, h]
 
-        def row_split(m, j):
-            w = groups[m][1]
-            g_rows, v_rows = FIRST if m < NFIRST else LAST if m >= len(groups) - NLAST else (G_ROWS, V_ROWS)
-            return NA + ((v_rows - NA) * w if j == 0 else 0), (H - 1) * NA - ((g_rows - NA) * w if j == w - 1 else 0)
-
-        def outer_rows(engine, m, j, h, b, i0, i1):
-            if i1 > i0:
-                shape = [P, PACK, i1 - i0, R]
-                engine.tensor_tensor(
-                    out=head_tile(m, h)[:, :, j, i0:i1, :],
-                    in0=b[:, h, :, j, :].unsqueeze(2).to_broadcast(shape),
-                    in1=an[m][:, h, j, i0:i1].unsqueeze(1).unsqueeze(3).to_broadcast(shape),
-                    op=ALU.mult)
-
         def outer_head(engine, m, h, b):
-            w = groups[m][1]
             engine.tensor_tensor(
                 out=head_tile(m, h)[:].rearrange("p t w i r -> p (t w i r)"),
-                in0=b[:, h, :, :, :].rearrange("p t w r -> p (t w) r").unsqueeze(2).to_broadcast([P, PACK * w, NA, R]),
-                in1=an[m][:, h, :, :].rearrange("p w i -> p (w i)").unsqueeze(1).unsqueeze(3).to_broadcast([P, PACK, w * NA, R]),
+                in0=b[:, h, :, :, :].rearrange("p t w r -> p (t w) r").unsqueeze(2).to_broadcast([P, PACK * W, NA, R]),
+                in1=a_norm[m][:, h, :, :].rearrange("p w i -> p (w i)").unsqueeze(1).unsqueeze(3)
+                .to_broadcast([P, PACK, W * NA, R]),
+                op=ALU.mult)
+
+        def outer_rows(engine, m, j, h, b, rows):
+            shape = [P, PACK, rows, R]
+            engine.tensor_tensor(
+                out=head_tile(m, h)[:, :, j, 0:rows, :],
+                in0=b[:, h, :, j, :].unsqueeze(2).to_broadcast(shape),
+                in1=a_norm[m][:, h, j, 0:rows].unsqueeze(1).unsqueeze(3).to_broadcast(shape),
                 op=ALU.mult)
 
         def outer_gpsimd(m):
-            w = groups[m][1]
-            outer_head(nc.gpsimd, m, 3, eb[m])
-            outer_rows(nc.gpsimd, m, w - 1, 2, eb[m], row_split(m, w - 1)[1] - 2 * NA, NA)
+            outer_head(nc.gpsimd, m, 3, exp_b[m])
+            outer_rows(nc.gpsimd, m, 1, 2, exp_b[m], NA)
 
-        def outer_vector(m, j):
-            if MERGE_V:
-                if j == 0:
-                    outer_head(nc.vector, m, 0, bps[m])
-            elif j < groups[m][1]:
-                outer_rows(nc.vector, m, j, 0, bps[m], 0, NA)
+        def outer_vector(m):
+            outer_head(nc.vector, m, 0, b_psum[m])
+            outer_rows(nc.vector, m, 0, 1, b_psum[m], VECTOR_ROWS)
 
-        def outer_vector_shared(m):
-            outer_rows(nc.vector, m, 0, 1, bps[m], 0, row_split(m, 0)[0] - NA)
+        def outer_scalar(m, j, h, first_row):
+            for i in range(first_row, NA):
+                nc.scalar.activation(out=head_tile(m, h)[:, :, j, i, :], in_=exp_b[m][:, h, :, j, :],
+                                     func=ACT.Copy, scale=a_norm[m][:, h, j, i:i + 1])
 
-        def outer_scalar(m, j, h):
-            if j < groups[m][1]:
-                lo, hi = row_split(m, j)
-                for i in range(max(lo - h * NA, 0), min(hi - h * NA, NA)):
-                    nc.scalar.activation(out=head_tile(m, h)[:, :, j, i, :], in_=eb[m][:, h, :, j, :],
-                                         func=ACT.Copy, scale=an[m][:, h, j, i:i + 1])
-
-        def turn_w(m, j, g):
-            if j < groups[m][1]:
-                wt[m, j, g] = ps4.tile([P, PACK, P], F32, name="wt")
-                for t in range(PACK):
-                    for h in range(H):
-                        nc.tensor.matmul(out=wt[m, j, g][:, t, :],
-                                         lhsT=prod[m, h][:, t, j, g * IG:(g + 1) * IG, :].rearrange("p i r -> p (i r)"),
-                                         rhs=ident[:], is_transpose=True, start=(h == 0), stop=(h == H - 1))
+        def turn_w(m):
+            for j in range(W):
+                for g in range(G):
+                    w_turned[m, j, g] = ps4.tile([P, PACK, P], F32, name="w_turned")
+                    for t in range(PACK):
+                        for h in range(H):
+                            nc.tensor.matmul(
+                                out=w_turned[m, j, g][:, t, :],
+                                lhsT=prod[m, h][:, t, j, g * IG:(g + 1) * IG, :].rearrange("p i r -> p (i r)"),
+                                rhs=ident[:], is_transpose=True, start=(h == 0), stop=(h == H - 1))
 
         def apply_gain(m, j, g):
-            w = groups[m][1]
-            if j < w:
-                if m not in ub:
-                    ub[m] = work.tile([P, w, G, P, PACK], BF16, name="ub", align_bytes=64)
-                nc.vector.tensor_tensor(out=ub[m][:, j, g, :, :], in0=wt[m, j, g][:].rearrange("p t k -> p k t"),
-                                        in1=gain[:, g, :].unsqueeze(1).to_broadcast([P, P, PACK]), op=ALU.mult)
+            if m not in u_bf:
+                u_bf[m] = work.tile([P, W, G, P, PACK], BF16, name="u_bf", align_bytes=64)
+            nc.vector.tensor_tensor(out=u_bf[m][:, j, g, :, :], in0=w_turned[m, j, g][:].rearrange("p t n -> p n t"),
+                                    in1=gain[:, g, :].unsqueeze(1).to_broadcast([P, P, PACK]), op=ALU.mult)
 
         def quantise_u(m):
-            w = groups[m][1]
-            uq[m] = work.tile([P, w * G * P], U32, name="uq", align_bytes=64)
-            uqs[m] = work.tile([P, w * G * P], U8, name="uqs", align_bytes=64)
-            nc.vector.quantize_mx(out=uq[m][:].bitcast(FP8X4), scales=uqs[m][:],
-                                  in_=ub[m][:].rearrange("p w g k t -> p (w g k t)"))
+            u_codes[m] = work.tile([P, W * G * P], U32, name="u_codes", align_bytes=64)
+            u_scales[m] = work.tile([P, W * G * P], U8, name="u_scales", align_bytes=64)
+            nc.vector.quantize_mx(out=u_codes[m][:].bitcast(FP8X4), scales=u_scales[m][:],
+                                  in_=u_bf[m][:].rearrange("p w g n t -> p (w g n t)"))
 
         def read_values(m):
-            for j in range(groups[m][1]):
+            for j in range(W):
                 for g in range(G):
                     tok = slice((j * G + g) * P, (j * G + g + 1) * P)
-                    nc.tensor.matmul_mx(out=r_of(m)[:, j, :], lhsT=uq[m][:, tok].bitcast(FP8X4), lhsT_scale=uqs[m][:, tok],
-                                        rhs=v_codes[:, g * V:(g + 1) * V].bitcast(FP8X4), rhs_scale=v_scales[:, g * V:(g + 1) * V],
-                                        start=(g == 0), stop=(g == G - 1))
+                    col = slice(g * V, (g + 1) * V)
+                    nc.tensor.matmul_mx(out=r_of(m)[:, j, :], lhsT=u_codes[m][:, tok].bitcast(FP8X4),
+                                        lhsT_scale=u_scales[m][:, tok], rhs=v_codes[:, col].bitcast(FP8X4),
+                                        rhs_scale=v_scales[:, col], start=(g == 0), stop=(g == G - 1))
 
         def finish(m):
-            n0, w = groups[m]
-            ot = work.tile([P, w, V], F32, name="ot")
-            nc.vector.scalar_tensor_tensor(out=ot[:], in0=r_of(m), scalar=0.5, in1=gt[m][:], op0=ALU.mult, op1=ALU.mult)
-            nc.sync.dma_start(out=out[n0 * P:(n0 + w) * P, :].rearrange("(p q) v -> p q v", q=w), in_=ot[:])
+            result = work.tile([P, W, V], F32, name="result")
+            nc.vector.scalar_tensor_tensor(out=result[:], in0=r_of(m), scalar=0.5, in1=gate[m][:],
+                                           op0=ALU.mult, op1=ALU.mult)
+            nc.sync.dma_start(out=tokens_of(out, m), in_=result[:])
 
         def on(stage, m, *more):
-            if 0 <= m < len(groups):
+            if 0 <= m < PAIRS:
                 stage(m, *more)
 
-        for s in range(-3, len(groups) + 3):
+        for s in range(-3, PAIRS + 3):
             on(quantise_x, s + 1)
             if s == -1:
                 quantise_weights(KEYS, KEYS + V)
@@ -296,33 +281,27 @@ def tile_denseproductkeymemorygated_t_kernel(tc, x_bytes, x_scale, ka, kb, gs, v
             on(normalise, s)
             on(outer_gpsimd, s)
             on(turn_x, s + 2)
-            on(logits, s + 1)
-            on(read_values, s - 3)
             on(b_to_psum, s)
-            on(turn_w, s - 1, 1, 0)
-            on(turn_w, s - 1, 1, 1)
-            on(widen, s + 3)
-            on(half_tanh, s + 1)
-            on(outer_scalar, s, 0, 1)
-            on(outer_scalar, s, 0, 2)
-            on(apply_gain, s - 1, 0, 0)
-            on(apply_gain, s - 1, 0, 1)
+            on(project, s + 1)
+            on(read_values, s - 3)
+            on(widen_x, s + 3)
+            on(tanh_z, s + 1)
+            on(outer_scalar, s, 0, 1, VECTOR_ROWS)
             on(row_max, s + 1)
             on(exps, s + 1)
-            on(outer_scalar, s, 1, 1)
-            on(outer_scalar, s, 1, 2)
-            on(outer_vector, s, 0)
-            on(outer_vector_shared, s)
-            on(turn_w, s, 0, 0)
-            on(turn_w, s, 0, 1)
+            on(outer_scalar, s, 0, 2, 0)
+            on(outer_scalar, s, 1, 1, 0)
+            on(turn_w, s - 1)
+            on(outer_vector, s)
             on(scale_x, s + 2)
             if s == -2:
                 quantise_weights(0, KEYS)
                 group_gate_weights()
             on(finish, s - 3)
-            on(apply_gain, s - 1, 1, 0)
-            on(apply_gain, s - 1, 1, 1)
-            on(outer_vector, s, 1)
-            on(sum_product, s + 1)
-            on(gate, s + 1)
+            on(apply_gain, s - 1, 0, 0)
+            on(multiply_sums, s + 1)
+            on(apply_gain, s - 1, 0, 1)
             on(invert, s + 1)
+            on(apply_gain, s - 1, 1, 0)
+            on(make_gate, s + 1)
+            on(apply_gain, s - 1, 1, 1)

@@ -25,7 +25,8 @@ W = 2
 PAIRS = T // (W * P)
 KEYS = H * NA + H * NB
 
-VECTOR_ROWS = 6
+GPSIMD_ROWS = 28
+VECTOR_ROWS = 4
 
 
 def tile_denseproductkeymemorygated_t_kernel(tc, x_bytes, x_scale, ka, kb, gs, vals, wg, out):
@@ -218,7 +219,7 @@ def tile_denseproductkeymemorygated_t_kernel(tc, x_bytes, x_scale, ka, kb, gs, v
 
         def outer_gpsimd(m):
             outer_head(nc.gpsimd, m, 3, exp_b[m])
-            outer_rows(nc.gpsimd, m, 1, 2, exp_b[m], NA)
+            outer_rows(nc.gpsimd, m, 1, 2, exp_b[m], GPSIMD_ROWS)
 
         def outer_vector(m):
             outer_head(nc.vector, m, 0, b_psum[m])
@@ -291,6 +292,7 @@ def tile_denseproductkeymemorygated_t_kernel(tc, x_bytes, x_scale, ka, kb, gs, v
             on(exps, s + 1)
             on(outer_scalar, s, 0, 2, 0)
             on(outer_scalar, s, 1, 1, 0)
+            on(outer_scalar, s, 1, 2, GPSIMD_ROWS)
             on(turn_w, s - 1)
             on(outer_vector, s)
             on(scale_x, s + 2)

from contextlib import ExitStack

import concourse.mybir as mybir
from concourse.masks import make_identity

T, D, H, NA, NB, V = 8192, 512, 4, 32, 32, 128
FLOPS = 2 * T * D * (H * NA + H * NB + V) + 2 * T * NA * NB * V

F32 = mybir.dt.float32
BF16 = mybir.dt.bfloat16
U32 = mybir.dt.uint32
U8 = mybir.dt.uint8
FP8 = mybir.dt.float8_e4m3fn
FP8X4 = mybir.dt.float8_e4m3fn_x4
ALU = mybir.AluOpType
ACT = mybir.ActivationFunctionType
AX = mybir.AxisListType

P = 128
PACK = 4
R = NB // PACK
G = NA * NB // (P * PACK)
IG = NA // G
W = 2
PAIRS = T // (W * P)
KEYS = H * NA + H * NB

GPSIMD_ROWS = 28
VECTOR_ROWS = 4


def tile_denseproductkeymemorygated_t_kernel(tc, x_bytes, x_scale, ka, kb, gs, vals, wg, out):
    nc = tc.nc
    with ExitStack() as ctx:
        keep = ctx.enter_context(tc.tile_pool(name="keep", bufs=1))
        xin = ctx.enter_context(tc.tile_pool(name="xin", bufs=PAIRS))
        work = ctx.enter_context(tc.tile_pool(name="work", bufs=3))
        prods = ctx.enter_context(tc.tile_pool(name="prods", bufs=3))
        gates = ctx.enter_context(tc.tile_pool(name="gates", bufs=6))
        ps1 = ctx.enter_context(tc.psum_pool(name="ps1", bufs=1))
        ps4 = ctx.enter_context(tc.psum_pool(name="ps4", bufs=W * G))
        ctx.enter_context(tc.manual_schedule())

        def tokens_of(dram, m):
            return dram[m * W * P:(m + 1) * W * P, :].rearrange("(p w) c -> p w c", w=W)

        xraw = {}

        def load_x(m):
            xraw[m] = xin.tile([P, W, D], U8, name="xraw")
            nc.sync.dma_start(out=xraw[m][:], in_=tokens_of(x_bytes, m))

        load_x(0)
        xs = keep.tile([P, PACK], F32, name="xs")
        nc.sync.dma_start(out=xs[:], in_=x_scale.rearrange("o (p t) -> p (o t)", t=PACK))
        ka_raw = keep.tile([P, PACK, H * NA], BF16, name="ka_raw")
        nc.sync.dma_start(out=ka_raw[:], in_=ka.rearrange("(p t) h i -> p t (h i)", t=PACK))
        kb_raw = keep.tile([P, PACK, H * NB], BF16, name="kb_raw")
        nc.sync.dma_start(out=kb_raw[:], in_=kb.rearrange("(p t) h j -> p t (h j)", t=PACK))
        load_x(1)
        wg_raw = keep.tile([P, PACK, V], BF16, name="wg_raw")
        nc.sync.dma_start(out=wg_raw[:], in_=wg.rearrange("(p t) v -> p t v", t=PACK))
        load_x(2)
        vals_raw = keep.tile([P, G, PACK * V], BF16, name="vals_raw")
        nc.sync.dma_start(out=vals_raw[:],
                          in_=vals.rearrange("i j v -> (i j) v").rearrange("(g p t) v -> p g (t v)", g=G, t=PACK))
        gain = keep.tile([P, G, PACK], BF16, name="gain")
        nc.sync.dma_start(out=gain[:], in_=gs.rearrange("i j -> (i j)").rearrange("(g p t) -> p g t", g=G, t=PACK))
        for m in range(3, PAIRS):
            load_x(m)

        ident = keep.tile([P, P], F32, name="ident")
        make_identity(nc, ident[:])

        w_grp = keep.tile([P, KEYS + V, PACK], BF16, name="w_grp", align_bytes=64)
        w_codes = keep.tile([P, KEYS + V], U32, name="w_codes", align_bytes=64)
        w_scales = keep.tile([P, KEYS + V], U8, name="w_scales", align_bytes=64)
        nc.vector.tensor_copy(out=w_grp[:, 0:H * NA, :], in_=ka_raw[:].rearrange("p t c -> p c t"))
        nc.vector.tensor_copy(
            out=w_grp[:, H * NA:KEYS, :].rearrange("p (h s r) t -> p h s r t", h=H, s=PACK),
            in_=kb_raw[:].rearrange("p t (h r s) -> p h s r t", h=H, s=PACK),
        )

        def group_gate_weights():
            nc.vector.tensor_copy(out=w_grp[:, KEYS:KEYS + V, :], in_=wg_raw[:].rearrange("p t c -> p c t"))

        def quantise_weights(lo, hi):
            nc.vector.quantize_mx(out=w_codes[:, lo:hi].bitcast(FP8X4), scales=w_scales[:, lo:hi],
                                  in_=w_grp[:, lo:hi, :].rearrange("p c t -> p (c t)"))

        v_grp = keep.tile([P, G, V, PACK], BF16, name="v_grp", align_bytes=64)
        v_codes = keep.tile([P, G * V], U32, name="v_codes", align_bytes=64)
        v_scales = keep.tile([P, G * V], U8, name="v_scales", align_bytes=64)

        def quantise_vals():
            nc.vector.tensor_copy(out=v_grp[:], in_=vals_raw[:].rearrange("p g (t v) -> p g v t", t=PACK))
            nc.vector.quantize_mx(out=v_codes[:].bitcast(FP8X4), scales=v_scales[:],
                                  in_=v_grp[:].rearrange("p g v t -> p (g v t)"))

        x_wide, x_turned, x_bf, x_codes, x_scales = {}, {}, {}, {}, {}
        logit, neg_max, exp_a, exp_b, sums, sum_prod, inv, a_norm, b_psum = {}, {}, {}, {}, {}, {}, {}, {}, {}
        half_tanh, gate, zr_bank = {}, {}, {}
        prod, w_turned, u_bf, u_codes, u_scales = {}, {}, {}, {}, {}

        def widen_x(m):
            x_wide[m] = work.tile([P, W, D], BF16, name="x_wide")
            nc.scalar.copy(out=x_wide[m][:], in_=xraw[m][:].bitcast(FP8))

        def turn_x(m):
            x_turned[m] = ps1.tile([P, 2, W * P], F32, name="x_turned")
            for j in range(W):
                words = x_wide[m][:, j, :].bitcast(F32)
                for u in range(2):
                    nc.tensor.transpose(x_turned[m][:, u, j * P:(j + 1) * P], words[:, u:D // 2:2], ident[:])

        def scale_x(m):
            shape = [P, W * P, 2, 2]
            x_bf[m] = work.tile(shape, BF16, name="x_bf", align_bytes=64)
            nc.vector.tensor_tensor(
                out=x_bf[m][:],
                in0=x_turned[m][:].rearrange("p u n -> p (u n)").bitcast(BF16).rearrange("p (u n e) -> p n u e", u=2, e=2),
                in1=xs[:].rearrange("p (u e) -> p u e", u=2).unsqueeze(1).to_broadcast(shape),
                op=ALU.mult)

        def quantise_x(m):
            x_codes[m] = work.tile([P, W * P], U32, name="x_codes", align_bytes=64)
            x_scales[m] = work.tile([P, W * P], U8, name="x_scales", align_bytes=64)
            nc.vector.quantize_mx(out=x_codes[m][:].bitcast(FP8X4), scales=x_scales[m][:],
                                  in_=x_bf[m][:].rearrange("p n u e -> p (n u e)"))

        def bank_of_step(s):
            if s not in zr_bank:
                zr_bank[s] = ps1.tile([P, 2, W, V], F32, name="zr_bank")
            return zr_bank[s]

        def z_of(m):
            return bank_of_step(m - 1)[:, 0, :, :]

        def r_of(m):
            return bank_of_step(m + 3)[:, 1, :, :]

        def project(m):
            logit[m] = ps1.tile([P, W, KEYS], F32, name="logit")
            for target, lo, hi in ((logit[m], 0, KEYS), (z_of(m), KEYS, KEYS + V)):
                for j in range(W):
                    tok = slice(j * P, (j + 1) * P)
                    nc.tensor.matmul_mx(out=target[:, j, :], lhsT=x_codes[m][:, tok].bitcast(FP8X4),
                                        lhsT_scale=x_scales[m][:, tok], rhs=w_codes[:, lo:hi].bitcast(FP8X4),
                                        rhs_scale=w_scales[:, lo:hi], start=True, stop=True)

        def row_max(m):
            neg_max[m] = work.tile([P, W * 2 * H], F32, name="neg_max")
            nc.vector.tensor_reduce(out=neg_max[m][:], in_=logit[m][:].rearrange("p w (c i) -> p (w c) i", i=NA),
                                    axis=AX.X, op=ALU.max, negate=True)

        def exps(m):
            exp_a[m] = work.tile([P, H, W, NA], F32, name="exp_a")
            exp_b[m] = work.tile([P, H, PACK, W, R], F32, name="exp_b")
            sums[m] = work.tile([P, 2, H, W], F32, name="sums")
            for j in range(W):
                for h in range(H):
                    targets = (exp_a[m][:, h, j, :].rearrange("p (t r) -> p t r", r=R), exp_b[m][:, h, :, j, :])
                    for half, target in enumerate(targets):
                        c = half * H + h
                        nc.scalar.activation(
                            out=target, in_=logit[m][:, j, c * NA:(c + 1) * NA].rearrange("p (t r) -> p t r", r=R),
                            func=ACT.Exp, bias=neg_max[m][:, j * 2 * H + c:j * 2 * H + c + 1],
                            accum_out=sums[m][:, half, h, j:j + 1])

        def tanh_z(m):
            half_tanh[m] = work.tile([P, W, V], F32, name="half_tanh")
            nc.scalar.activation(out=half_tanh[m][:], in_=z_of(m), func=ACT.Tanh, scale=0.5)

        def make_gate(m):
            gate[m] = gates.tile([P, W, V], F32, name="gate")
            nc.vector.scalar_tensor_tensor(out=gate[m][:], in0=half_tanh[m][:], scalar=1.0, in1=z_of(m),
                                           op0=ALU.add, op1=ALU.mult)

        def multiply_sums(m):
            sum_prod[m] = work.tile([P, H * W], F32, name="sum_prod")
            nc.vector.tensor_reduce(out=sum_prod[m][:], in_=sums[m][:].rearrange("p u h w -> p (h w) u"),
                                    axis=AX.X, op=ALU.mult)

        def invert(m):
            inv[m] = work.tile([P, H * W], F32, name="inv")
            nc.vector.reciprocal(out=inv[m][:], in_=sum_prod[m][:])

        def normalise(m):
            a_norm[m] = work.tile([P, H, W, NA], F32, name="a_norm")
            nc.vector.tensor_tensor(out=a_norm[m][:].rearrange("p h w i -> p (h w) i"),
                                    in0=exp_a[m][:].rearrange("p h w i -> p (h w) i"),
                                    in1=inv[m][:].unsqueeze(2).to_broadcast([P, H * W, NA]), op=ALU.mult)

        def b_to_psum(m):
            b_psum[m] = ps1.tile([P, H, PACK, W, R], F32, name="b_psum")
            nc.tensor.matmul(out=b_psum[m][:].rearrange("p h t w r -> p (h t w r)"), lhsT=ident[:],
                             rhs=exp_b[m][:].rearrange("p h t w r -> p (h t w r)"), start=True, stop=True)

        def head_tile(m, h):
            if (m, h) not in prod:
                prod[m, h] = prods.tile([P, PACK, W, NA, R], F32, name="prod%d" % h)
            return prod[m, h]

        def outer_head(engine, m, h, b):
            engine.tensor_tensor(
                out=head_tile(m, h)[:].rearrange("p t w i r -> p (t w i r)"),
                in0=b[:, h, :, :, :].rearrange("p t w r -> p (t w) r").unsqueeze(2).to_broadcast([P, PACK * W, NA, R]),
                in1=a_norm[m][:, h, :, :].rearrange("p w i -> p (w i)").unsqueeze(1).unsqueeze(3)
                .to_broadcast([P, PACK, W * NA, R]),
                op=ALU.mult)

        def outer_rows(engine, m, j, h, b, rows):
            shape = [P, PACK, rows, R]
            engine.tensor_tensor(
                out=head_tile(m, h)[:, :, j, 0:rows, :],
                in0=b[:, h, :, j, :].unsqueeze(2).to_broadcast(shape),
                in1=a_norm[m][:, h, j, 0:rows].unsqueeze(1).unsqueeze(3).to_broadcast(shape),
                op=ALU.mult)

        def outer_gpsimd(m):
            outer_head(nc.gpsimd, m, 3, exp_b[m])
            outer_rows(nc.gpsimd, m, 1, 2, exp_b[m], GPSIMD_ROWS)

        def outer_vector(m):
            outer_head(nc.vector, m, 0, b_psum[m])
            outer_rows(nc.vector, m, 0, 1, b_psum[m], VECTOR_ROWS)

        def outer_scalar(m, j, h, first_row):
            for i in range(first_row, NA):
                nc.scalar.activation(out=head_tile(m, h)[:, :, j, i, :], in_=exp_b[m][:, h, :, j, :],
                                     func=ACT.Copy, scale=a_norm[m][:, h, j, i:i + 1])

        def turn_w(m):
            for j in range(W):
                for g in range(G):
                    w_turned[m, j, g] = ps4.tile([P, PACK, P], F32, name="w_turned")
                    for t in range(PACK):
                        for h in range(H):
                            nc.tensor.matmul(
                                out=w_turned[m, j, g][:, t, :],
                                lhsT=prod[m, h][:, t, j, g * IG:(g + 1) * IG, :].rearrange("p i r -> p (i r)"),
                                rhs=ident[:], is_transpose=True, start=(h == 0), stop=(h == H - 1))

        def apply_gain(m, j, g):
            if m not in u_bf:
                u_bf[m] = work.tile([P, W, G, P, PACK], BF16, name="u_bf", align_bytes=64)
            nc.vector.tensor_tensor(out=u_bf[m][:, j, g, :, :], in0=w_turned[m, j, g][:].rearrange("p t n -> p n t"),
                                    in1=gain[:, g, :].unsqueeze(1).to_broadcast([P, P, PACK]), op=ALU.mult)

        def quantise_u(m):
            u_codes[m] = work.tile([P, W * G * P], U32, name="u_codes", align_bytes=64)
            u_scales[m] = work.tile([P, W * G * P], U8, name="u_scales", align_bytes=64)
            nc.vector.quantize_mx(out=u_codes[m][:].bitcast(FP8X4), scales=u_scales[m][:],
                                  in_=u_bf[m][:].rearrange("p w g n t -> p (w g n t)"))

        def read_values(m):
            for j in range(W):
                for g in range(G):
                    tok = slice((j * G + g) * P, (j * G + g + 1) * P)
                    col = slice(g * V, (g + 1) * V)
                    nc.tensor.matmul_mx(out=r_of(m)[:, j, :], lhsT=u_codes[m][:, tok].bitcast(FP8X4),
                                        lhsT_scale=u_scales[m][:, tok], rhs=v_codes[:, col].bitcast(FP8X4),
                                        rhs_scale=v_scales[:, col], start=(g == 0), stop=(g == G - 1))

        def finish(m):
            result = work.tile([P, W, V], F32, name="result")
            nc.vector.scalar_tensor_tensor(out=result[:], in0=r_of(m), scalar=0.5, in1=gate[m][:],
                                           op0=ALU.mult, op1=ALU.mult)
            nc.sync.dma_start(out=tokens_of(out, m), in_=result[:])

        def on(stage, m, *more):
            if 0 <= m < PAIRS:
                stage(m, *more)

        for s in range(-3, PAIRS + 3):
            on(quantise_x, s + 1)
            if s == -1:
                quantise_weights(KEYS, KEYS + V)
            on(quantise_u, s - 2)
            if s == 1:
                quantise_vals()
            on(normalise, s)
            on(outer_gpsimd, s)
            on(turn_x, s + 2)
            on(b_to_psum, s)
            on(project, s + 1)
            on(read_values, s - 3)
            on(widen_x, s + 3)
            on(tanh_z, s + 1)
            on(outer_scalar, s, 0, 1, VECTOR_ROWS)
            on(row_max, s + 1)
            on(exps, s + 1)
            on(outer_scalar, s, 0, 2, 0)
            on(outer_scalar, s, 1, 1, 0)
            on(outer_scalar, s, 1, 2, GPSIMD_ROWS)
            on(turn_w, s - 1)
            on(outer_vector, s)
            on(scale_x, s + 2)
            if s == -2:
                quantise_weights(0, KEYS)
                group_gate_weights()
            on(finish, s - 3)
            on(apply_gain, s - 1, 0, 0)
            on(multiply_sums, s + 1)
            on(apply_gain, s - 1, 0, 1)
            on(invert, s + 1)
            on(apply_gain, s - 1, 1, 0)
            on(make_gate, s + 1)
            on(apply_gain, s - 1, 1, 1)
